import numpy as np
import ml_dtypes


def mxq(x, axis, fmt="e4m3"):
    dtype, down = {"e4m3": (ml_dtypes.float8_e4m3fn, 7), "e5m2": (ml_dtypes.float8_e5m2, 14)}[fmt]
    v = np.moveaxis(np.asarray(x, np.float32).astype(ml_dtypes.bfloat16).astype(np.float64), axis, -1)
    blocks = v.reshape(v.shape[:-1] + (-1, 32))
    amax = np.abs(blocks).max(-1, keepdims=True)
    byte = np.maximum(np.where(amax > 0, np.frexp(amax)[1] - 1 + 127, 0) - down, 1)
    scale = np.exp2(byte - 127.0)
    codes = (blocks / scale).astype(np.float32).astype(dtype).astype(np.float64)
    return np.moveaxis((codes * scale).reshape(v.shape), -1, axis)


WIDE = False


def mx_kscale(k):
    if not WIDE:
        return np.ones(k)
    levels = np.array([18, -18])
    if k % 512:
        return np.exp2(np.random.permutation(np.resize(levels, k // 32))).repeat(32)
    a = np.empty((k // 512, 16))
    for p in range(k // 512):
        a[p, :8] = np.random.permutation(np.resize(levels, 8))
        for g in range(8):
            far = levels[np.abs(levels - a[p, g]) >= 10]
            a[p, g + 8] = far[np.random.randint(len(far))]
    return np.exp2(a.ravel()).repeat(32)


def f64(x):
    return np.asarray(x).astype(np.float64)


def striped(idx):
    return np.tile(np.asarray(idx).reshape(-1, 16).T, (8, 1)).astype(np.uint16)


def unstriped(offs):
    return offs[:16].T.reshape(-1).astype(np.int64)


T, C, D, DV = 1024, 512, 512, 512
BETA = 0.25


def setup_inputs():
    n = np.random.standard_normal
    grid = lambda v: np.clip(np.round(v * 16) / 16, -4, 4)
    v = mx_kscale(DV)[:, None]
    return {
        "zT": (grid(n((DV, T))) * v).astype(np.float32),
        "cb": (grid(n((DV, C))) * v).astype(np.float32),
        "cb2": (grid(0.5 * n((DV, C))) * v).astype(np.float32),
        "dyT": (grid(0.5 * n((DV, T))) * v).astype(np.float32),
        "wm": (n((DV, D)) / np.sqrt(DV) / v).astype(np.float32),
        "offs": striped(np.random.randint(0, C, T)),
        "offs2": striped(np.random.randint(0, C, T)),
    }


def reference(zT, cb, cb2, dyT, wm, offs, offs2):
    e = f64(zT) - f64(cb)[:, unstriped(offs)] - f64(cb2)[:, unstriped(offs2)]
    g = (f64(dyT) + BETA * e)
    return mxq(f64(wm), 0, "e4m3").T @ mxq(g, 0, "e5m2")

@@ -1,0 +1,273 @@
+from contextlib import ExitStack
+
+import concourse.mybir as mybir
+from concourse.masks import make_identity
+
+T, C, D, DV = 1024, 512, 512, 512
+BETA = 0.25
+FLOPS = 2 * DV * D * T
+
+F32 = mybir.dt.float32
+BF16 = mybir.dt.bfloat16
+U32 = mybir.dt.uint32
+U16 = mybir.dt.uint16
+U8 = mybir.dt.uint8
+E4 = mybir.dt.float8_e4m3fn_x4
+E5 = mybir.dt.float8_e5m2_x4
+SUB = mybir.AluOpType.subtract
+ADD = mybir.AluOpType.add
+COPY = mybir.ActivationFunctionType.Copy
+
+P = 128
+PACK = 4
+QT = 256
+HT = 512
+WINDOW = (1024, 576)
+
+
+def tile_attend_gvq_rs_x_kernel(tc, zT, cb, cb2, dyT, wm, offs, offs2, out):
+    nc = tc.nc
+    with ExitStack() as ctx:
+        keep = ctx.enter_context(tc.tile_pool(name="keep", bufs=1))
+        psum = ctx.enter_context(tc.psum_pool(name="psum", bufs=1))
+
+        ident = keep.tile([P, P], F32, name="ident")
+        make_identity(nc, ident[:])
+
+        z_pl = zT.rearrange("(p j) t -> p j t", j=PACK)
+        dy_pl = dyT.rearrange("(p j) t -> p j t", j=PACK)
+        books = [cb.rearrange("(p j) c -> p j c", j=PACK), cb2.rearrange("(p j) c -> p j c", j=PACK)]
+        lists_hbm = [offs, offs2]
+
+        lists = {}
+        book = {}
+        z_sb = {}
+        dy_sb = {}
+        dy4 = {}
+        diff = {}
+        pair_words = {}
+        back = {}
+
+        def load_list(b):
+            lists[b] = keep.tile([P, T // 16], U16, name="list%d" % b)
+            nc.sync.dma_start(lists[b][:], lists_hbm[b])
+
+        def load_book(b, j):
+            book[b, j] = keep.tile([P, WINDOW[b]], F32, name="book%d_%d" % (b, j))
+            nc.vector.memset(book[b, j][:, C:], 0.0)
+            nc.sync.dma_start(book[b, j][:, :C], books[b][:, j, :])
+
+        def load_z(j, q0, nq):
+            z_tile = keep.tile([P, nq * QT], F32, name="z%d_%d" % (j, q0))
+            nc.sync.dma_start(z_tile[:], z_pl[:, j, q0 * QT:(q0 + nq) * QT])
+            z_sb[j, 2 * q0] = z_tile
+            for i in range(1, nq):
+                z_sb[j, 2 * (q0 + i)] = z_tile[:, i * QT:(i + 1) * QT]
+
+        def load_dy(j, h):
+            dy_sb[j, h] = keep.tile([P, HT], F32, name="dy%d_%d" % (j, h), tag="dy%d_%d" % (j, h), align_bytes=64)
+            nc.sync.dma_start(dy_sb[j, h][:], dy_pl[:, j, h * HT:(h + 1) * HT])
+
+        w_raw = keep.tile([P, PACK, D], F32, name="w_raw")
+
+        load_book(0, 0)
+        load_list(0)
+        load_z(0, 0, 1)
+        load_z(0, 1, 1)
+        load_z(0, 2, 2)
+        load_dy(0, 0)
+        load_list(1)
+        load_book(1, 0)
+        load_dy(0, 1)
+        load_book(0, 1)
+        load_z(1, 0, 2)
+        load_dy(1, 0)
+        load_book(1, 1)
+        load_z(1, 2, 2)
+        load_dy(1, 1)
+        load_book(0, 2)
+        load_z(2, 0, 2)
+        nc.sync.dma_start(w_raw[:], wm.rearrange("(p j) d -> p j d", j=PACK))
+        load_book(0, 3)
+        load_z(3, 0, 2)
+        load_dy(2, 0)
+        load_book(1, 2)
+        load_dy(3, 0)
+        load_book(1, 3)
+        load_dy(2, 1)
+        load_z(2, 2, 2)
+        load_dy(3, 1)
+        load_z(3, 2, 2)
+
+        def scale_dy(j, h):
+            scaled = keep.tile([P, HT], F32, name="dy4_%d_%d" % (j, h))
+            nc.scalar.activation(out=scaled[:], in_=dy_sb[j, h][:], func=COPY, scale=-1.0 / BETA)
+            for i in range(4):
+                dy4[j, 4 * h + i] = scaled[:, i * P:]
+
+        def gather(b, j, tb0, ntb, into=None):
+            width = ntb * P
+            if into is None:
+                fresh = keep.tile([P, width], F32, name="diff%d_%d_%d" % (b, j, tb0))
+                into = fresh[:]
+            for i in range(ntb):
+                diff[b, j, tb0 + i] = into[:, i * P:(i + 1) * P]
+            window = book[b, j][:].indirect(lists[b][:, tb0 * (P // 16):(tb0 + ntb) * (P // 16)])
+            nc.vector.tensor_tensor(into, window, (z_sb, dy4)[b][j, tb0][:, :width], (SUB, ADD)[b])
+
+        def add_up(u, tb0, ntb, bank_tag, into=None, on_vector=False):
+            bank = psum.tile([P, ntb, 2, P], F32, name="sum%d_%d" % (u, tb0), tag=bank_tag)
+            for e in range(2):
+                for i in range(ntb):
+                    for b in range(2):
+                        nc.tensor.matmul(
+                            bank[:, i, e, :],
+                            lhsT=diff[b, 2 * u + e, tb0 + i],
+                            rhs=ident[:],
+                            is_transpose=True,
+                            start=(b == 0),
+                            stop=(b == 1),
+                        )
+            if into is None:
+                fresh = keep.tile([P, ntb * 2 * P], BF16, name="pairs%d_%d" % (u, tb0))
+                into = fresh[:]
+            for i in range(ntb):
+                pair_words[u, tb0 + i] = into[:, i * 2 * P:(i + 1) * 2 * P]
+            dst = into.rearrange("t (b p e) -> t b p e", b=ntb, e=2)
+            src = bank[:].rearrange("t b e p -> t b p e")
+            if on_vector:
+                nc.vector.tensor_scalar_mul(dst, src, -BETA)
+            else:
+                nc.scalar.activation(out=dst, in_=src, func=COPY, scale=-BETA)
+
+        def turn_back(u, tb0, ntb, bank_tag=None):
+            if u == 0:
+                back[tb0] = psum.tile([P, 2, ntb * P], F32, name="back%d" % tb0, tag=bank_tag)
+            for i in range(ntb):
+                nc.tensor.transpose(back[tb0][:, u, i * P:(i + 1) * P], pair_words[u, tb0 + i].bitcast(F32), ident[:])
+
+        g_codes = [keep.tile([P, HT], U32, name="g_codes%d" % h, align_bytes=64) for h in range(2)]
+        g_scales = [keep.tile([P, HT], U8, name="g_scales%d" % h, align_bytes=64) for h in range(2)]
+        g_bf = {}
+
+        def weave(tb0, ntb, on_vector=False):
+            g_bf[tb0] = keep.tile([P, ntb * P * PACK], BF16, name="g_bf%d" % tb0, tag="g_bf%d" % tb0, align_bytes=64)
+            dst = g_bf[tb0][:].bitcast(F32).rearrange("p (t u) -> p t u", u=2)
+            src = back[tb0][:].rearrange("p u t -> p t u")
+            if on_vector:
+                nc.vector.tensor_copy(out=dst, in_=src)
+            else:
+                nc.scalar.copy(out=dst, in_=src)
+
+        def quantise_g(tb0, ntb):
+            h = tb0 // 4
+            cols = slice((tb0 % 4) * P, (tb0 % 4 + ntb) * P)
+            nc.vector.quantize_mx(out=g_codes[h][:, cols].bitcast(E5), scales=g_scales[h][:, cols], in_=g_bf[tb0][:])
+
+        w_bf = {}
+        w_codes = keep.tile([P, D], U32, name="w_codes", align_bytes=64)
+        w_scales = keep.tile([P, D], U8, name="w_scales", align_bytes=64)
+
+        def cast_w(m, tag):
+            w_bf[m] = keep.tile([P, P * PACK], BF16, name="w_bf%d" % m, tag=tag, align_bytes=64)
+            nc.scalar.copy(
+                out=w_bf[m][:].rearrange("p (c i j) -> p c j i", i=4, j=PACK),
+                in_=w_raw[:, :, m * P:(m + 1) * P].rearrange("p j (c i) -> p c j i", i=4),
+            )
+
+        def quantise_w(m):
+            cols = slice(m * P, (m + 1) * P)
+            nc.vector.quantize_mx(out=w_codes[:, cols].bitcast(E4), scales=w_scales[:, cols], in_=w_bf[m][:])
+
+        def multiply(h, m, bank_tag, on_vector):
+            acc = psum.tile([P, HT], F32, name="acc%d_%d" % (h, m), tag=bank_tag)
+            nc.tensor.matmul_mx(
+                out=acc[:],
+                lhsT=w_codes[:, m * P:(m + 1) * P].bitcast(E4),
+                lhsT_scale=w_scales[:, m * P:(m + 1) * P],
+                rhs=g_codes[h][:].bitcast(E5),
+                rhs_scale=g_scales[h][:],
+                start=True,
+                stop=True,
+            )
+            res = keep.tile([P, HT], F32, name="res%d_%d" % (h, m))
+            if on_vector:
+                nc.vector.tensor_copy(out=res[:], in_=acc[:])
+            else:
+                nc.scalar.copy(out=res[:], in_=acc[:])
+            nc.sync.dma_start(out[m * P:(m + 1) * P, h * HT:(h + 1) * HT], res[:])
+
+        scale_dy(0, 0)
+        scale_dy(0, 1)
+        gather(0, 0, 0, 2)
+        gather(0, 0, 2, 2)
+        gather(0, 0, 4, 4)
+        gather(1, 0, 0, 4)
+        gather(1, 0, 4, 4)
+        scale_dy(1, 0)
+        scale_dy(1, 1)
+        first_pairs = keep.tile([P, 2, 2 * QT], BF16, name="first_pairs", tag="dy1_1", align_bytes=64)
+        for h in range(2):
+            for b in range(2):
+                gather(b, 1, 4 * h, 4)
+            for q in (2 * h, 2 * h + 1):
+                add_up(0, 2 * q, 2, "sum%d" % (q % 2), first_pairs[:, q, :] if h == 0 else None)
+                if q < 3:
+                    turn_back(0, 2 * q, 2, "back%d" % q)
+        turn_back(0, 6, 1, "back3")
+        turn_back(0, 7, 1, "back4")
+        cast_w(0, "w_bf0")
+        scale_dy(2, 0)
+        cast_w(1, "dy2_0")
+        scale_dy(3, 0)
+        cast_w(2, "dy3_0")
+        scale_dy(2, 1)
+        for b in range(2):
+            for j in (2, 3):
+                if (b, j) == (1, 3):
+                    gather(b, j, 0, 2)
+                    gather(b, j, 2, 2)
+                else:
+                    gather(b, j, 0, 4)
+                if b == 0:
+                    quantise_w(j - 2)
+        add_up(1, 0, 2, "sum0")
+        turn_back(1, 0, 2)
+        scale_dy(3, 1)
+        late_pairs = keep.tile([P, 2 * QT], BF16, name="late_pairs", tag="dy3_1", align_bytes=64)
+        add_up(1, 2, 2, "sum1", late_pairs[:])
+        turn_back(1, 2, 2)
+        weave(0, 2)
+        weave(2, 2)
+        cast_w(3, "dy2_1")
+        for j in (2, 3):
+            for b in range(2):
+                gather(b, j, 4, 2)
+        quantise_w(2)
+        quantise_w(3)
+        add_up(1, 4, 2, "sum1")
+        turn_back(1, 4, 2)
+        gather(0, 2, 6, 2)
+        quantise_g(0, 2)
+        quantise_g(2, 2)
+        multiply(0, 0, "out0", False)
+        weave(4, 2)
+        multiply(0, 1, "sum0", False)
+        last_diffs = keep.tile([P, 3, QT], F32, name="last_diffs", tag="g_bf2", align_bytes=64)
+        gather(1, 2, 6, 2, last_diffs[:, 0, :])
+        gather(0, 3, 6, 2, last_diffs[:, 1, :])
+        for i in range(2):
+            gather(1, 3, 6 + i, 1, last_diffs[:, 2, i * P:(i + 1) * P])
+        multiply(0, 2, "back0", False)
+        multiply(0, 3, "back1", False)
+        add_up(1, 6, 1, "sum1", None, True)
+        add_up(1, 7, 1, "out0", None, True)
+        quantise_g(4, 2)
+        for tb in (6, 7):
+            turn_back(1, tb, 1)
+        for tb in (6, 7):
+            weave(tb, 1, True)
+        for tb in (6, 7):
+            quantise_g(tb, 1)
+        for m, tag in enumerate(("sum0", "back2", "back0", "back1")):
+            multiply(1, m, tag, m % 2 == 1)

@@ -16,6 +16,7 @@ E4 = mybir.dt.float8_e4m3fn_x4
 E5 = mybir.dt.float8_e5m2_x4
 SUB = mybir.AluOpType.subtract
 ADD = mybir.AluOpType.add
+MULT = mybir.AluOpType.mult
 COPY = mybir.ActivationFunctionType.Copy
 
 P = 128
@@ -47,6 +48,7 @@ def tile_attend_gvq_rs_x_kernel(tc, zT, cb, cb2, dyT, wm, offs, offs2, out):
         diff = {}
         pair_words = {}
         back = {}
+        words = {}
 
         def load_list(b):
             lists[b] = keep.tile([P, T // 16], U16, name="list%d" % b)
@@ -60,52 +62,56 @@ def tile_attend_gvq_rs_x_kernel(tc, zT, cb, cb2, dyT, wm, offs, offs2, out):
         def load_z(j, q0, nq):
             z_tile = keep.tile([P, nq * QT], F32, name="z%d_%d" % (j, q0))
             nc.sync.dma_start(z_tile[:], z_pl[:, j, q0 * QT:(q0 + nq) * QT])
-            z_sb[j, 2 * q0] = z_tile
-            for i in range(1, nq):
-                z_sb[j, 2 * (q0 + i)] = z_tile[:, i * QT:(i + 1) * QT]
+            for i in range(2 * nq):
+                z_sb[j, 2 * q0 + i] = z_tile[:, i * P:]
 
-        def load_dy(j, h):
-            dy_sb[j, h] = keep.tile([P, HT], F32, name="dy%d_%d" % (j, h), tag="dy%d_%d" % (j, h), align_bytes=64)
-            nc.sync.dma_start(dy_sb[j, h][:], dy_pl[:, j, h * HT:(h + 1) * HT])
+        def load_dy(j, q0, nq):
+            dy_sb[j, q0] = keep.tile([P, nq * QT], F32, name="dy%d_%d" % (j, q0), tag="dy%d_%d" % (j, q0), align_bytes=64)
+            nc.sync.dma_start(dy_sb[j, q0][:], dy_pl[:, j, q0 * QT:(q0 + nq) * QT])
+
+        def load_pair(name, planes, u):
+            pair = keep.tile([P, 2, HT], F32, name=name, tag=name, align_bytes=64)
+            nc.sync.dma_start(pair[:], planes[:, 2 * u:2 * u + 2, HT:])
+            return pair
+
+        def load_w(j0=0, nj=4):
+            nc.sync.dma_start(w_raw[:, j0:j0 + nj, :], wm.rearrange("(p j) d -> p j d", j=PACK)[:, j0:j0 + nj, :])
 
         w_raw = keep.tile([P, PACK, D], F32, name="w_raw")
 
         load_book(0, 0)
         load_list(0)
-        load_z(0, 0, 1)
-        load_z(0, 1, 1)
-        load_z(0, 2, 2)
-        load_dy(0, 0)
+        load_z(0, 2, 1)
+        load_z(0, 3, 1)
+        load_z(0, 0, 2)
         load_list(1)
         load_book(1, 0)
-        load_dy(0, 1)
+        load_dy(0, 0, 2)
         load_book(0, 1)
-        load_z(1, 0, 2)
-        load_dy(1, 0)
-        load_book(1, 1)
         load_z(1, 2, 2)
-        load_dy(1, 1)
+        load_z(1, 0, 2)
+        load_book(1, 1)
+        load_dy(1, 0, 2)
         load_book(0, 2)
         load_z(2, 0, 2)
-        nc.sync.dma_start(w_raw[:], wm.rearrange("(p j) d -> p j d", j=PACK))
+        load_dy(2, 0, 2)
+        load_dy(3, 0, 2)
+        load_book(1, 2)
+        dy_low = load_pair("dy_low", dy_pl, 0)
         load_book(0, 3)
         load_z(3, 0, 2)
-        load_dy(2, 0)
-        load_book(1, 2)
-        load_dy(3, 0)
+        load_w()
         load_book(1, 3)
-        load_dy(2, 1)
-        load_z(2, 2, 2)
-        load_dy(3, 1)
-        load_z(3, 2, 2)
+        z_high = load_pair("z_high", z_pl, 1)
+        dy_high = load_pair("dy_high", dy_pl, 1)
 
-        def scale_dy(j, h):
-            scaled = keep.tile([P, HT], F32, name="dy4_%d_%d" % (j, h))
-            nc.scalar.activation(out=scaled[:], in_=dy_sb[j, h][:], func=COPY, scale=-1.0 / BETA)
-            for i in range(4):
-                dy4[j, 4 * h + i] = scaled[:, i * P:]
+        def scale_dy(j, q0, first, nq):
+            scaled = keep.tile([P, nq * QT], F32, name="dy4_%d_%d" % (j, q0 + first), tag="dy4_%d_%d" % (j, q0 + first), align_bytes=64)
+            nc.scalar.activation(out=scaled[:], in_=dy_sb[j, q0][:, first * QT:(first + nq) * QT], func=COPY, scale=-1.0 / BETA)
+            for i in range(2 * nq):
+                dy4[j, 2 * (q0 + first) + i] = scaled[:, i * P:]
 
-        def gather(b, j, tb0, ntb, into=None):
+        def gather(b, j, tb0, ntb, into=None, other=None):
             width = ntb * P
             if into is None:
                 fresh = keep.tile([P, width], F32, name="diff%d_%d_%d" % (b, j, tb0))
@@ -113,20 +119,22 @@ def tile_attend_gvq_rs_x_kernel(tc, zT, cb, cb2, dyT, wm, offs, offs2, out):
             for i in range(ntb):
                 diff[b, j, tb0 + i] = into[:, i * P:(i + 1) * P]
             window = book[b, j][:].indirect(lists[b][:, tb0 * (P // 16):(tb0 + ntb) * (P // 16)])
-            nc.vector.tensor_tensor(into, window, (z_sb, dy4)[b][j, tb0][:, :width], (SUB, ADD)[b])
+            if other is None:
+                other = (z_sb, dy4)[b][j, tb0][:, :width]
+            nc.vector.tensor_tensor(into, window, other, (SUB, ADD)[b])
 
-        def add_up(u, tb0, ntb, bank_tag, into=None, on_vector=False):
+        def add_up(u, tb0, ntb, bank_tag, into=None, on_vector=False, order=(1, 0), planes=(1, 0)):
             bank = psum.tile([P, ntb, 2, P], F32, name="sum%d_%d" % (u, tb0), tag=bank_tag)
-            for e in range(2):
+            for e in planes:
                 for i in range(ntb):
-                    for b in range(2):
+                    for b in order:
                         nc.tensor.matmul(
                             bank[:, i, e, :],
                             lhsT=diff[b, 2 * u + e, tb0 + i],
                             rhs=ident[:],
                             is_transpose=True,
-                            start=(b == 0),
-                            stop=(b == 1),
+                            start=(b == order[0]),
+                            stop=(b == order[1]),
                         )
             if into is None:
                 fresh = keep.tile([P, ntb * 2 * P], BF16, name="pairs%d_%d" % (u, tb0))
@@ -146,7 +154,30 @@ def tile_attend_gvq_rs_x_kernel(tc, zT, cb, cb2, dyT, wm, offs, offs2, out):
             for i in range(ntb):
                 nc.tensor.transpose(back[tb0][:, u, i * P:(i + 1) * P], pair_words[u, tb0 + i].bitcast(F32), ident[:])
 
-        g_codes = [keep.tile([P, HT], U32, name="g_codes%d" % h, align_bytes=64) for h in range(2)]
+        def keep_words(tb0, ntb, first):
+            words[tb0] = keep.tile([P, 2, ntb * P], F32, name="words%d" % tb0)
+            nc.scalar.copy(out=words[tb0][:, 0, :], in_=back[first][:, 0, (tb0 - first) * P:(tb0 - first + ntb) * P])
+
+        def pair_up(u, tb0, ntb, minus_e, dy_pair):
+            nc.vector.scalar_tensor_tensor(
+                out=words[tb0][:, u, :].bitcast(BF16).rearrange("p (t e) -> p t e", e=2),
+                in0=minus_e.rearrange("p e t -> p t e"),
+                scalar=-BETA,
+                in1=dy_pair.rearrange("p e t -> p t e"),
+                op0=MULT,
+                op1=ADD,
+            )
+
+        def weave_words(tb0, ntb, on_vector):
+            g_bf[tb0] = keep.tile([P, ntb * P * PACK], BF16, name="g_bf%d" % tb0, align_bytes=64)
+            dst = g_bf[tb0][:].bitcast(F32).rearrange("p (t u) -> p t u", u=2)
+            src = words[tb0][:].rearrange("p u t -> p t u")
+            if on_vector:
+                nc.vector.tensor_copy(out=dst, in_=src)
+            else:
+                nc.scalar.copy(out=dst, in_=src)
+
+        g_codes = {}
         g_scales = [keep.tile([P, HT], U8, name="g_scales%d" % h, align_bytes=64) for h in range(2)]
         g_bf = {}
 
@@ -164,20 +195,14 @@ def tile_attend_gvq_rs_x_kernel(tc, zT, cb, cb2, dyT, wm, offs, offs2, out):
             cols = slice((tb0 % 4) * P, (tb0 % 4 + ntb) * P)
             nc.vector.quantize_mx(out=g_codes[h][:, cols].bitcast(E5), scales=g_scales[h][:, cols], in_=g_bf[tb0][:])
 
-        w_bf = {}
-        w_codes = keep.tile([P, D], U32, name="w_codes", align_bytes=64)
+        w_bf = keep.tile([P, D * PACK], BF16, name="w_bf", tag="w_bf", align_bytes=64)
         w_scales = keep.tile([P, D], U8, name="w_scales", align_bytes=64)
 
-        def cast_w(m, tag):
-            w_bf[m] = keep.tile([P, P * PACK], BF16, name="w_bf%d" % m, tag=tag, align_bytes=64)
+        def cast_w(m):
             nc.scalar.copy(
-                out=w_bf[m][:].rearrange("p (c i j) -> p c j i", i=4, j=PACK),
+                out=w_bf[:, m * P * PACK:(m + 1) * P * PACK].rearrange("p (c i j) -> p c j i", i=4, j=PACK),
                 in_=w_raw[:, :, m * P:(m + 1) * P].rearrange("p j (c i) -> p c j i", i=4),
             )
-
-        def quantise_w(m):
-            cols = slice(m * P, (m + 1) * P)
-            nc.vector.quantize_mx(out=w_codes[:, cols].bitcast(E4), scales=w_scales[:, cols], in_=w_bf[m][:])
 
         def multiply(h, m, bank_tag, on_vector):
             acc = psum.tile([P, HT], F32, name="acc%d_%d" % (h, m), tag=bank_tag)
@@ -197,77 +222,70 @@ def tile_attend_gvq_rs_x_kernel(tc, zT, cb, cb2, dyT, wm, offs, offs2, out):
                 nc.scalar.copy(out=res[:], in_=acc[:])
             nc.sync.dma_start(out[m * P:(m + 1) * P, h * HT:(h + 1) * HT], res[:])
 
-        scale_dy(0, 0)
-        scale_dy(0, 1)
-        gather(0, 0, 0, 2)
-        gather(0, 0, 2, 2)
-        gather(0, 0, 4, 4)
+        scale_dy(0, 0, 0, 2)
+        scale_dy(1, 0, 0, 2)
+        part_low = keep.tile([P, 2, HT], F32, name="part_low")
+        minus_e_low = keep.tile([P, 2, HT], F32, name="minus_e_low")
+        gather(0, 0, 4, 2, part_low[:, 0, :QT])
+        gather(0, 0, 6, 2, part_low[:, 0, QT:])
+        gather(0, 0, 0, 4)
+        gather(1, 0, 4, 4, minus_e_low[:, 0, :], part_low[:, 0, :])
         gather(1, 0, 0, 4)
-        gather(1, 0, 4, 4)
-        scale_dy(1, 0)
-        scale_dy(1, 1)
-        first_pairs = keep.tile([P, 2, 2 * QT], BF16, name="first_pairs", tag="dy1_1", align_bytes=64)
-        for h in range(2):
-            for b in range(2):
-                gather(b, 1, 4 * h, 4)
-            for q in (2 * h, 2 * h + 1):
-                add_up(0, 2 * q, 2, "sum%d" % (q % 2), first_pairs[:, q, :] if h == 0 else None)
-                if q < 3:
-                    turn_back(0, 2 * q, 2, "back%d" % q)
-        turn_back(0, 6, 1, "back3")
-        turn_back(0, 7, 1, "back4")
-        cast_w(0, "w_bf0")
-        scale_dy(2, 0)
-        cast_w(1, "dy2_0")
-        scale_dy(3, 0)
-        cast_w(2, "dy3_0")
-        scale_dy(2, 1)
-        for b in range(2):
-            for j in (2, 3):
-                if (b, j) == (1, 3):
-                    gather(b, j, 0, 2)
-                    gather(b, j, 2, 2)
-                else:
-                    gather(b, j, 0, 4)
-                if b == 0:
-                    quantise_w(j - 2)
-        add_up(1, 0, 2, "sum0")
-        turn_back(1, 0, 2)
-        scale_dy(3, 1)
-        late_pairs = keep.tile([P, 2 * QT], BF16, name="late_pairs", tag="dy3_1", align_bytes=64)
-        add_up(1, 2, 2, "sum1", late_pairs[:])
-        turn_back(1, 2, 2)
+        gather(0, 1, 4, 4, part_low[:, 1, :])
+        gather(0, 1, 0, 4)
+        gather(1, 1, 4, 4, minus_e_low[:, 1, :], part_low[:, 1, :])
+        gather(1, 1, 0, 4)
+        scale_dy(2, 0, 0, 2)
+        scale_dy(3, 0, 0, 2)
+        low_pairs = keep.tile([P, 2, 2 * QT], BF16, name="low_pairs", tag="dy3_0", align_bytes=64)
+        for q in range(2):
+            add_up(0, 2 * q, 2, "sum%d" % q, low_pairs[:, q, :], False, (0, 1), (0, 1))
+            turn_back(0, 2 * q, 2, "back%d" % q)
+        gather(0, 2, 0, 4)
+        gather(1, 2, 0, 4)
+        for m in range(4):
+            cast_w(m)
+        for tb0, ntb in ((4, 2), (6, 1), (7, 1)):
+            words[tb0] = keep.tile([P, 2, ntb * P], F32, name="words%d" % tb0)
+            cols = slice((tb0 - 4) * P, (tb0 - 4 + ntb) * P)
+            pair_up(0, tb0, ntb, minus_e_low[:, :, cols], dy_low[:, :, cols])
+        gather(0, 3, 0, 4)
+        gather(1, 3, 0, 2)
+        gather(1, 3, 2, 2)
+        for q in range(2):
+            add_up(1, 2 * q, 2, "sum%d" % q, None, False, (0, 1), (0, 1))
+            turn_back(1, 2 * q, 2)
         weave(0, 2)
         weave(2, 2)
-        cast_w(3, "dy2_1")
-        for j in (2, 3):
-            for b in range(2):
-                gather(b, j, 4, 2)
-        quantise_w(2)
-        quantise_w(3)
-        add_up(1, 4, 2, "sum1")
-        turn_back(1, 4, 2)
-        gather(0, 2, 6, 2)
+        part2 = keep.tile([P, 2, QT], F32, name="part2", tag="part2", align_bytes=64)
+        minus_e2 = keep.tile([P, 2, QT], F32, name="minus_e2")
+        for e in range(2):
+            gather(0, 2 + e, 4, 2, part2[:, e, :], z_high[:, e, :QT])
+        for e in range(2):
+            gather(1, 2 + e, 4, 2, minus_e2[:, e, :], part2[:, e, :])
+        w_codes = keep.tile([P, D], U32, name="w_codes", tag="part2", align_bytes=64)
+        nc.vector.quantize_mx(out=w_codes[:].bitcast(E4), scales=w_scales[:], in_=w_bf[:])
+        g_codes[0] = keep.tile([P, HT], U32, name="g_codes0", align_bytes=64)
         quantise_g(0, 2)
+        pair_up(1, 4, 2, minus_e2[:], dy_high[:, :, :QT])
         quantise_g(2, 2)
-        multiply(0, 0, "out0", False)
-        weave(4, 2)
-        multiply(0, 1, "sum0", False)
-        last_diffs = keep.tile([P, 3, QT], F32, name="last_diffs", tag="g_bf2", align_bytes=64)
-        gather(1, 2, 6, 2, last_diffs[:, 0, :])
-        gather(0, 3, 6, 2, last_diffs[:, 1, :])
+        weave_words(4, 2, False)
+        part3 = keep.tile([P, 2, QT], F32, name="part3", tag="g_bf2", align_bytes=64)
+        minus_e3 = keep.tile([P, 2, QT], F32, name="minus_e3")
+        for e in range(2):
+            gather(0, 2 + e, 6, 2, part3[:, e, :], z_high[:, e, QT:])
+        gather(1, 2, 6, 2, minus_e3[:, 0, :], part3[:, 0, :])
         for i in range(2):
-            gather(1, 3, 6 + i, 1, last_diffs[:, 2, i * P:(i + 1) * P])
-        multiply(0, 2, "back0", False)
-        multiply(0, 3, "back1", False)
-        add_up(1, 6, 1, "sum1", None, True)
-        add_up(1, 7, 1, "out0", None, True)
+            gather(1, 3, 6 + i, 1, minus_e3[:, 1, i * P:(i + 1) * P], part3[:, 1, i * P:(i + 1) * P])
+        for i in range(2):
+            pair_up(1, 6 + i, 1, minus_e3[:, :, i * P:(i + 1) * P], dy_high[:, :, QT + i * P:QT + (i + 1) * P])
+        g_codes[1] = keep.tile([P, HT], U32, name="g_codes1", tag="z_high", align_bytes=64)
+        for i in range(2):
+            weave_words(6 + i, 1, True)
         quantise_g(4, 2)
-        for tb in (6, 7):
-            turn_back(1, tb, 1)
-        for tb in (6, 7):
-            weave(tb, 1, True)
-        for tb in (6, 7):
-            quantise_g(tb, 1)
-        for m, tag in enumerate(("sum0", "back2", "back0", "back1")):
-            multiply(1, m, tag, m % 2 == 1)
+        for i in range(2):
+            quantise_g(6 + i, 1)
+        for m in range(4):
+            multiply(0, m, "out%d" % m, False)
+        for m, tag in enumerate(("sum0", "sum1", "back0", "back1")):
+            multiply(1, m, tag, m % 2 == 0)

@@ -69,41 +69,47 @@ def tile_attend_gvq_rs_x_kernel(tc, zT, cb, cb2, dyT, wm, offs, offs2, out):
             dy_sb[j, q0] = keep.tile([P, nq * QT], F32, name="dy%d_%d" % (j, q0), tag="dy%d_%d" % (j, q0), align_bytes=64)
             nc.sync.dma_start(dy_sb[j, q0][:], dy_pl[:, j, q0 * QT:(q0 + nq) * QT])
 
-        def load_pair(name, planes, u):
-            pair = keep.tile([P, 2, HT], F32, name=name, tag=name, align_bytes=64)
-            nc.sync.dma_start(pair[:], planes[:, 2 * u:2 * u + 2, HT:])
+        def load_pair(name, planes, u, q0, nq):
+            pair = keep.tile([P, 2, nq * QT], F32, name=name, tag=name, align_bytes=64)
+            nc.sync.dma_start(pair[:], planes[:, 2 * u:2 * u + 2, q0 * QT:(q0 + nq) * QT])
             return pair
 
-        def load_w(j0=0, nj=4):
-            nc.sync.dma_start(w_raw[:, j0:j0 + nj, :], wm.rearrange("(p j) d -> p j d", j=PACK)[:, j0:j0 + nj, :])
+        w_raw = {}
 
-        w_raw = keep.tile([P, PACK, D], F32, name="w_raw")
+        def load_w(h):
+            w_raw[h] = keep.tile([P, PACK, D // 2], F32, name="w_half%d" % h, tag="w_half%d" % h, align_bytes=64)
+            nc.sync.dma_start(w_raw[h][:], wm.rearrange("(p j) d -> p j d", j=PACK)[:, :, h * (D // 2):(h + 1) * (D // 2)])
+
 
         load_book(0, 0)
         load_list(0)
-        load_z(0, 2, 1)
-        load_z(0, 3, 1)
-        load_z(0, 0, 2)
+        load_z(0, 0, 1)
+        load_z(0, 1, 1)
+        load_z(0, 2, 2)
+        load_dy(0, 0, 2)
         load_list(1)
         load_book(1, 0)
-        load_dy(0, 0, 2)
+        load_dy(0, 2, 2)
         load_book(0, 1)
-        load_z(1, 2, 2)
         load_z(1, 0, 2)
-        load_book(1, 1)
         load_dy(1, 0, 2)
+        load_book(1, 1)
+        load_z(1, 2, 2)
+        load_dy(1, 2, 2)
         load_book(0, 2)
         load_z(2, 0, 2)
         load_dy(2, 0, 2)
-        load_dy(3, 0, 2)
         load_book(1, 2)
-        dy_low = load_pair("dy_low", dy_pl, 0)
         load_book(0, 3)
         load_z(3, 0, 2)
-        load_w()
+        load_dy(3, 0, 2)
         load_book(1, 3)
-        z_high = load_pair("z_high", z_pl, 1)
-        dy_high = load_pair("dy_high", dy_pl, 1)
+        load_w(0)
+        z_third = load_pair("z_third", z_pl, 1, 2, 1)
+        dy_third = load_pair("dy_third", dy_pl, 1, 2, 1)
+        load_w(1)
+        z_last = load_pair("z_last", z_pl, 1, 3, 1)
+        dy_last = load_pair("dy_last", dy_pl, 1, 3, 1)
 
         def scale_dy(j, q0, first, nq):
             scaled = keep.tile([P, nq * QT], F32, name="dy4_%d_%d" % (j, q0 + first), tag="dy4_%d_%d" % (j, q0 + first), align_bytes=64)
@@ -181,8 +187,8 @@ def tile_attend_gvq_rs_x_kernel(tc, zT, cb, cb2, dyT, wm, offs, offs2, out):
         g_scales = [keep.tile([P, HT], U8, name="g_scales%d" % h, align_bytes=64) for h in range(2)]
         g_bf = {}
 
-        def weave(tb0, ntb, on_vector=False):
-            g_bf[tb0] = keep.tile([P, ntb * P * PACK], BF16, name="g_bf%d" % tb0, tag="g_bf%d" % tb0, align_bytes=64)
+        def weave(tb0, ntb, tag=None, on_vector=False):
+            g_bf[tb0] = keep.tile([P, ntb * P * PACK], BF16, name="g_bf%d" % tb0, tag=tag or "g_bf%d" % tb0, align_bytes=64)
             dst = g_bf[tb0][:].bitcast(F32).rearrange("p (t u) -> p t u", u=2)
             src = back[tb0][:].rearrange("p u t -> p t u")
             if on_vector:
@@ -195,20 +201,35 @@ def tile_attend_gvq_rs_x_kernel(tc, zT, cb, cb2, dyT, wm, offs, offs2, out):
             cols = slice((tb0 % 4) * P, (tb0 % 4 + ntb) * P)
             nc.vector.quantize_mx(out=g_codes[h][:, cols].bitcast(E5), scales=g_scales[h][:, cols], in_=g_bf[tb0][:])
 
-        w_bf = keep.tile([P, D * PACK], BF16, name="w_bf", tag="w_bf", align_bytes=64)
+        w_bf = {}
+        w_codes = {}
         w_scales = keep.tile([P, D], U8, name="w_scales", align_bytes=64)
 
-        def cast_w(m):
+        def cast_w(m, tag=None):
+            h, half = divmod(m, 2)
+            if half == 0:
+                w_bf[h] = keep.tile([P, 2 * P * PACK], BF16, name="w_bf%d" % h, tag=tag or "w_bf%d" % h, align_bytes=64)
             nc.scalar.copy(
-                out=w_bf[:, m * P * PACK:(m + 1) * P * PACK].rearrange("p (c i j) -> p c j i", i=4, j=PACK),
-                in_=w_raw[:, :, m * P:(m + 1) * P].rearrange("p j (c i) -> p c j i", i=4),
+                out=w_bf[h][:, half * P * PACK:(half + 1) * P * PACK].rearrange("p (c i j) -> p c j i", i=4, j=PACK),
+                in_=w_raw[h][:, :, half * P:(half + 1) * P].rearrange("p j (c i) -> p c j i", i=4),
             )
+
+        def quantise_w(m0, nm, tag=None):
+            codes = keep.tile([P, nm * P], U32, name="w_codes%d" % m0, tag=tag or "w_codes%d" % m0, align_bytes=64)
+            first = (m0 % 2) * P * PACK
+            nc.vector.quantize_mx(
+                out=codes[:].bitcast(E4),
+                scales=w_scales[:, m0 * P:(m0 + nm) * P],
+                in_=w_bf[m0 // 2][:, first:first + nm * P * PACK],
+            )
+            for i in range(nm):
+                w_codes[m0 + i] = codes[:, i * P:(i + 1) * P]
 
         def multiply(h, m, bank_tag, on_vector):
             acc = psum.tile([P, HT], F32, name="acc%d_%d" % (h, m), tag=bank_tag)
             nc.tensor.matmul_mx(
                 out=acc[:],
-                lhsT=w_codes[:, m * P:(m + 1) * P].bitcast(E4),
+                lhsT=w_codes[m].bitcast(E4),
                 lhsT_scale=w_scales[:, m * P:(m + 1) * P],
                 rhs=g_codes[h][:].bitcast(E5),
                 rhs_scale=g_scales[h][:],
@@ -223,69 +244,77 @@ def tile_attend_gvq_rs_x_kernel(tc, zT, cb, cb2, dyT, wm, offs, offs2, out):
             nc.sync.dma_start(out[m * P:(m + 1) * P, h * HT:(h + 1) * HT], res[:])
 
         scale_dy(0, 0, 0, 2)
+        scale_dy(0, 2, 0, 2)
         scale_dy(1, 0, 0, 2)
-        part_low = keep.tile([P, 2, HT], F32, name="part_low")
-        minus_e_low = keep.tile([P, 2, HT], F32, name="minus_e_low")
-        gather(0, 0, 4, 2, part_low[:, 0, :QT])
-        gather(0, 0, 6, 2, part_low[:, 0, QT:])
-        gather(0, 0, 0, 4)
-        gather(1, 0, 4, 4, minus_e_low[:, 0, :], part_low[:, 0, :])
+        scale_dy(1, 2, 0, 2)
+        gather(0, 0, 0, 2)
+        gather(0, 0, 2, 2)
+        gather(0, 0, 4, 4)
         gather(1, 0, 0, 4)
-        gather(0, 1, 4, 4, part_low[:, 1, :])
+        gather(1, 0, 4, 4)
         gather(0, 1, 0, 4)
-        gather(1, 1, 4, 4, minus_e_low[:, 1, :], part_low[:, 1, :])
         gather(1, 1, 0, 4)
-        scale_dy(2, 0, 0, 2)
-        scale_dy(3, 0, 0, 2)
-        low_pairs = keep.tile([P, 2, 2 * QT], BF16, name="low_pairs", tag="dy3_0", align_bytes=64)
+        gather(0, 1, 4, 4)
+        gather(1, 1, 4, 4)
+        low_pairs = keep.tile([P, 2, 2 * QT], BF16, name="low_pairs", tag="dy1_2", align_bytes=64)
         for q in range(2):
-            add_up(0, 2 * q, 2, "sum%d" % q, low_pairs[:, q, :], False, (0, 1), (0, 1))
+            add_up(0, 2 * q, 2, "out%d" % q, low_pairs[:, q, :], False, (0, 1), (0, 1))
             turn_back(0, 2 * q, 2, "back%d" % q)
+        scale_dy(2, 0, 0, 2)
+        low_pairs2 = keep.tile([P, 2, 2 * QT], BF16, name="low_pairs2", tag="dy2_0", align_bytes=64)
+        for q in range(2, 4):
+            add_up(0, 2 * q, 2, "sum%d" % (q - 2), low_pairs2[:, q - 2, :], False, (0, 1), (0, 1))
+        turn_back(0, 4, 2, "back2")
+        turn_back(0, 6, 2, "back3")
+        scale_dy(3, 0, 0, 2)
+        keep_words(6, 1, 6)
+        keep_words(7, 1, 6)
+        cast_w(0)
+        cast_w(1)
         gather(0, 2, 0, 4)
         gather(1, 2, 0, 4)
-        for m in range(4):
-            cast_w(m)
-        for tb0, ntb in ((4, 2), (6, 1), (7, 1)):
-            words[tb0] = keep.tile([P, 2, ntb * P], F32, name="words%d" % tb0)
-            cols = slice((tb0 - 4) * P, (tb0 - 4 + ntb) * P)
-            pair_up(0, tb0, ntb, minus_e_low[:, :, cols], dy_low[:, :, cols])
         gather(0, 3, 0, 4)
         gather(1, 3, 0, 2)
         gather(1, 3, 2, 2)
+        high_pairs = keep.tile([P, 2, 2 * QT], BF16, name="high_pairs", tag="w_half0", align_bytes=64)
         for q in range(2):
-            add_up(1, 2 * q, 2, "sum%d" % q, None, False, (0, 1), (0, 1))
+            add_up(1, 2 * q, 2, ("sum1", "back3")[q], high_pairs[:, q, :], False, (1, 0), (0, 1))
             turn_back(1, 2 * q, 2)
-        weave(0, 2)
+        late4 = keep.tile([P, 2, QT], F32, name="late4", tag="late4", align_bytes=64)
+        nc.scalar.activation(out=late4[:], in_=dy_third[:], func=COPY, scale=-1.0 / BETA)
+        weave(0, 2, "dy_third")
         weave(2, 2)
-        part2 = keep.tile([P, 2, QT], F32, name="part2", tag="part2", align_bytes=64)
-        minus_e2 = keep.tile([P, 2, QT], F32, name="minus_e2")
         for e in range(2):
-            gather(0, 2 + e, 4, 2, part2[:, e, :], z_high[:, e, :QT])
+            gather(0, 2 + e, 4, 2, None, z_third[:, e, :])
+        quantise_w(0, 2, "dy4_3_0")
         for e in range(2):
-            gather(1, 2 + e, 4, 2, minus_e2[:, e, :], part2[:, e, :])
-        w_codes = keep.tile([P, D], U32, name="w_codes", tag="part2", align_bytes=64)
-        nc.vector.quantize_mx(out=w_codes[:].bitcast(E4), scales=w_scales[:], in_=w_bf[:])
-        g_codes[0] = keep.tile([P, HT], U32, name="g_codes0", align_bytes=64)
+            gather(1, 2 + e, 4, 2, None, late4[:, e, :])
+        add_up(1, 4, 2, "back3", None, False, (1, 0), (0, 1))
+        turn_back(1, 4, 2)
+        weave(4, 2)
+        cast_w(2, "w_half0")
+        cast_w(3)
+        part = keep.tile([P, 2, QT], F32, name="part")
+        for e in range(2):
+            gather(0, 2 + e, 6, 2, part[:, e, :], z_last[:, e, :])
+        g_codes[0] = keep.tile([P, HT], U32, name="g_codes0", tag="late4", align_bytes=64)
         quantise_g(0, 2)
-        pair_up(1, 4, 2, minus_e2[:], dy_high[:, :, :QT])
         quantise_g(2, 2)
-        weave_words(4, 2, False)
-        part3 = keep.tile([P, 2, QT], F32, name="part3", tag="g_bf2", align_bytes=64)
-        minus_e3 = keep.tile([P, 2, QT], F32, name="minus_e3")
-        for e in range(2):
-            gather(0, 2 + e, 6, 2, part3[:, e, :], z_high[:, e, QT:])
-        gather(1, 2, 6, 2, minus_e3[:, 0, :], part3[:, 0, :])
+        quantise_w(2, 1)
+        minus_e3 = keep.tile([P, 2, QT], F32, name="minus_e3", tag="g_bf2", align_bytes=64)
+        gather(1, 2, 6, 2, minus_e3[:, 0, :], part[:, 0, :])
         for i in range(2):
-            gather(1, 3, 6 + i, 1, minus_e3[:, 1, i * P:(i + 1) * P], part3[:, 1, i * P:(i + 1) * P])
+            gather(1, 3, 6 + i, 1, minus_e3[:, 1, i * P:(i + 1) * P], part[:, 1, i * P:(i + 1) * P])
+        quantise_w(3, 1)
         for i in range(2):
-            pair_up(1, 6 + i, 1, minus_e3[:, :, i * P:(i + 1) * P], dy_high[:, :, QT + i * P:QT + (i + 1) * P])
-        g_codes[1] = keep.tile([P, HT], U32, name="g_codes1", tag="z_high", align_bytes=64)
+            pair_up(1, 6 + i, 1, minus_e3[:, :, i * P:(i + 1) * P], dy_last[:, :, i * P:(i + 1) * P])
+        g_codes[1] = keep.tile([P, HT], U32, name="g_codes1", align_bytes=64)
         for i in range(2):
             weave_words(6 + i, 1, True)
         quantise_g(4, 2)
         for i in range(2):
             quantise_g(6 + i, 1)
-        for m in range(4):
-            multiply(0, m, "out%d" % m, False)
-        for m, tag in enumerate(("sum0", "sum1", "back0", "back1")):
+        for m, tag in enumerate(("out0", "back3", "out1", "sum0")):
+            multiply(0, m, tag, False)
+        for m, tag in enumerate(("sum1", "back0", "back1", "back2")):
             multiply(1, m, tag, m % 2 == 0)

@@ -74,17 +74,15 @@ def tile_attend_gvq_rs_x_kernel(tc, zT, cb, cb2, dyT, wm, offs, offs2, out):
             nc.sync.dma_start(pair[:], planes[:, 2 * u:2 * u + 2, q0 * QT:(q0 + nq) * QT])
             return pair
 
-        w_raw = {}
+        w_raw = keep.tile([P, PACK, D], F32, name="w_raw")
 
-        def load_w(h):
-            w_raw[h] = keep.tile([P, PACK, D // 2], F32, name="w_half%d" % h, tag="w_half%d" % h, align_bytes=64)
-            nc.sync.dma_start(w_raw[h][:], wm.rearrange("(p j) d -> p j d", j=PACK)[:, :, h * (D // 2):(h + 1) * (D // 2)])
+        def load_w():
+            nc.sync.dma_start(w_raw[:], wm.rearrange("(p j) d -> p j d", j=PACK))
 
 
         load_book(0, 0)
         load_list(0)
-        load_z(0, 0, 1)
-        load_z(0, 1, 1)
+        load_z(0, 0, 2)
         load_z(0, 2, 2)
         load_dy(0, 0, 2)
         load_list(1)
@@ -100,16 +98,13 @@ def tile_attend_gvq_rs_x_kernel(tc, zT, cb, cb2, dyT, wm, offs, offs2, out):
         load_z(2, 0, 2)
         load_dy(2, 0, 2)
         load_book(1, 2)
+        load_dy(3, 0, 2)
         load_book(0, 3)
         load_z(3, 0, 2)
-        load_dy(3, 0, 2)
         load_book(1, 3)
-        load_w(0)
-        z_third = load_pair("z_third", z_pl, 1, 2, 1)
-        dy_third = load_pair("dy_third", dy_pl, 1, 2, 1)
-        load_w(1)
-        z_last = load_pair("z_last", z_pl, 1, 3, 1)
-        dy_last = load_pair("dy_last", dy_pl, 1, 3, 1)
+        z_high = load_pair("z_high", z_pl, 1, 2, 2)
+        load_w()
+        dy_high = load_pair("dy_high", dy_pl, 1, 2, 2)
 
         def scale_dy(j, q0, first, nq):
             scaled = keep.tile([P, nq * QT], F32, name="dy4_%d_%d" % (j, q0 + first), tag="dy4_%d_%d" % (j, q0 + first), align_bytes=64)
@@ -205,22 +200,19 @@ def tile_attend_gvq_rs_x_kernel(tc, zT, cb, cb2, dyT, wm, offs, offs2, out):
         w_codes = {}
         w_scales = keep.tile([P, D], U8, name="w_scales", align_bytes=64)
 
-        def cast_w(m, tag=None):
-            h, half = divmod(m, 2)
-            if half == 0:
-                w_bf[h] = keep.tile([P, 2 * P * PACK], BF16, name="w_bf%d" % h, tag=tag or "w_bf%d" % h, align_bytes=64)
+        def cast_w(m):
             nc.scalar.copy(
-                out=w_bf[h][:, half * P * PACK:(half + 1) * P * PACK].rearrange("p (c i j) -> p c j i", i=4, j=PACK),
-                in_=w_raw[h][:, :, half * P:(half + 1) * P].rearrange("p j (c i) -> p c j i", i=4),
+                out=w_bf[0][:, m * P * PACK:(m + 1) * P * PACK].rearrange("p (c i j) -> p c j i", i=4, j=PACK),
+                in_=w_raw[:, :, m * P:(m + 1) * P].rearrange("p j (c i) -> p c j i", i=4),
             )
 
         def quantise_w(m0, nm, tag=None):
             codes = keep.tile([P, nm * P], U32, name="w_codes%d" % m0, tag=tag or "w_codes%d" % m0, align_bytes=64)
-            first = (m0 % 2) * P * PACK
+            first = m0 * P * PACK
             nc.vector.quantize_mx(
                 out=codes[:].bitcast(E4),
                 scales=w_scales[:, m0 * P:(m0 + nm) * P],
-                in_=w_bf[m0 // 2][:, first:first + nm * P * PACK],
+                in_=w_bf[0][:, first:first + nm * P * PACK],
             )
             for i in range(nm):
                 w_codes[m0 + i] = codes[:, i * P:(i + 1) * P]
@@ -247,8 +239,7 @@ def tile_attend_gvq_rs_x_kernel(tc, zT, cb, cb2, dyT, wm, offs, offs2, out):
         scale_dy(0, 2, 0, 2)
         scale_dy(1, 0, 0, 2)
         scale_dy(1, 2, 0, 2)
-        gather(0, 0, 0, 2)
-        gather(0, 0, 2, 2)
+        gather(0, 0, 0, 4)
         gather(0, 0, 4, 4)
         gather(1, 0, 0, 4)
         gather(1, 0, 4, 4)
@@ -267,54 +258,55 @@ def tile_attend_gvq_rs_x_kernel(tc, zT, cb, cb2, dyT, wm, offs, offs2, out):
         turn_back(0, 4, 2, "back2")
         turn_back(0, 6, 2, "back3")
         scale_dy(3, 0, 0, 2)
+        keep_words(4, 2, 4)
         keep_words(6, 1, 6)
         keep_words(7, 1, 6)
-        cast_w(0)
-        cast_w(1)
         gather(0, 2, 0, 4)
         gather(1, 2, 0, 4)
         gather(0, 3, 0, 4)
         gather(1, 3, 0, 2)
         gather(1, 3, 2, 2)
-        high_pairs = keep.tile([P, 2, 2 * QT], BF16, name="high_pairs", tag="w_half0", align_bytes=64)
+        high_pairs = keep.tile([P, 2, 2 * QT], BF16, name="high_pairs", tag="high_pairs", align_bytes=64)
         for q in range(2):
-            add_up(1, 2 * q, 2, ("sum1", "back3")[q], high_pairs[:, q, :], False, (1, 0), (0, 1))
+            add_up(1, 2 * q, 2, "out%d" % q, high_pairs[:, q, :], False, (1, 0), (0, 1))
             turn_back(1, 2 * q, 2)
-        late4 = keep.tile([P, 2, QT], F32, name="late4", tag="late4", align_bytes=64)
-        nc.scalar.activation(out=late4[:], in_=dy_third[:], func=COPY, scale=-1.0 / BETA)
-        weave(0, 2, "dy_third")
+        weave(0, 2)
         weave(2, 2)
+        w_bf[0] = keep.tile([P, D * PACK], BF16, name="w_bf", tag="high_pairs", align_bytes=64)
+        part = keep.tile([P, 2, HT], F32, name="part")
         for e in range(2):
-            gather(0, 2 + e, 4, 2, None, z_third[:, e, :])
-        quantise_w(0, 2, "dy4_3_0")
+            gather(0, 2 + e, 4, 4, part[:, e, :], z_high[:, e, :])
+        minus_third = keep.tile([P, 2, QT], F32, name="minus_third")
         for e in range(2):
-            gather(1, 2 + e, 4, 2, None, late4[:, e, :])
-        add_up(1, 4, 2, "back3", None, False, (1, 0), (0, 1))
-        turn_back(1, 4, 2)
-        weave(4, 2)
-        cast_w(2, "w_half0")
-        cast_w(3)
-        part = keep.tile([P, 2, QT], F32, name="part")
-        for e in range(2):
-            gather(0, 2 + e, 6, 2, part[:, e, :], z_last[:, e, :])
-        g_codes[0] = keep.tile([P, HT], U32, name="g_codes0", tag="late4", align_bytes=64)
+            gather(1, 2 + e, 4, 2, minus_third[:, e, :], part[:, e, :QT])
+        g_codes[0] = keep.tile([P, HT], U32, name="g_codes0", tag="z_high", align_bytes=64)
         quantise_g(0, 2)
         quantise_g(2, 2)
+        minus_last = keep.tile([P, 2, QT], F32, name="minus_last")
+        cast_w(0)
+        quantise_w(0, 1)
+        cast_w(1)
+        quantise_w(1, 1)
+        gather(1, 2, 6, 2, minus_last[:, 0, :], part[:, 0, QT:])
+        for i in range(2):
+            gather(1, 3, 6 + i, 1, minus_last[:, 1, i * P:(i + 1) * P], part[:, 1, QT + i * P:QT + (i + 1) * P])
+        multiply(0, 0, "sum0", False)
+        cast_w(2)
         quantise_w(2, 1)
-        minus_e3 = keep.tile([P, 2, QT], F32, name="minus_e3", tag="g_bf2", align_bytes=64)
-        gather(1, 2, 6, 2, minus_e3[:, 0, :], part[:, 0, :])
-        for i in range(2):
-            gather(1, 3, 6 + i, 1, minus_e3[:, 1, i * P:(i + 1) * P], part[:, 1, i * P:(i + 1) * P])
+        multiply(0, 1, "sum1", False)
+        cast_w(3)
         quantise_w(3, 1)
+        pair_up(1, 4, 2, minus_third[:], dy_high[:, :, :QT])
         for i in range(2):
-            pair_up(1, 6 + i, 1, minus_e3[:, :, i * P:(i + 1) * P], dy_last[:, :, i * P:(i + 1) * P])
+            pair_up(1, 6 + i, 1, minus_last[:, :, i * P:(i + 1) * P], dy_high[:, :, QT + i * P:QT + (i + 1) * P])
         g_codes[1] = keep.tile([P, HT], U32, name="g_codes1", align_bytes=64)
+        weave_words(4, 2, True)
         for i in range(2):
             weave_words(6 + i, 1, True)
         quantise_g(4, 2)
         for i in range(2):
             quantise_g(6 + i, 1)
-        for m, tag in enumerate(("out0", "back3", "out1", "sum0")):
-            multiply(0, m, tag, False)
-        for m, tag in enumerate(("sum1", "back0", "back1", "back2")):
+        multiply(0, 2, "back2", False)
+        multiply(0, 3, "back3", False)
+        for m, tag in enumerate(("out0", "out1", "back0", "back1")):
             multiply(1, m, tag, m % 2 == 0)

@@ -12,301 +12,271 @@ BF16 = mybir.dt.bfloat16
 U32 = mybir.dt.uint32
 U16 = mybir.dt.uint16
 U8 = mybir.dt.uint8
-E4 = mybir.dt.float8_e4m3fn_x4
-E5 = mybir.dt.float8_e5m2_x4
+E4M3X4 = mybir.dt.float8_e4m3fn_x4
+E5M2X4 = mybir.dt.float8_e5m2_x4
 SUB = mybir.AluOpType.subtract
 ADD = mybir.AluOpType.add
 MULT = mybir.AluOpType.mult
 COPY = mybir.ActivationFunctionType.Copy
 
 P = 128
-PACK = 4
-QT = 256
-HT = 512
-WINDOW = (1024, 576)
+PLANES = 4
+QUARTER = 256
+HALF = 512
+LIST_ROWS = 16
+WINDOW = (2 * C, C + 64)
 
 
 def tile_attend_gvq_rs_x_kernel(tc, zT, cb, cb2, dyT, wm, offs, offs2, out):
     nc = tc.nc
     with ExitStack() as ctx:
-        keep = ctx.enter_context(tc.tile_pool(name="keep", bufs=1))
+        sbuf = ctx.enter_context(tc.tile_pool(name="sbuf", bufs=1))
         psum = ctx.enter_context(tc.psum_pool(name="psum", bufs=1))
 
-        ident = keep.tile([P, P], F32, name="ident")
+        ident = sbuf.tile([P, P], F32, name="ident")
         make_identity(nc, ident[:])
 
-        z_pl = zT.rearrange("(p j) t -> p j t", j=PACK)
-        dy_pl = dyT.rearrange("(p j) t -> p j t", j=PACK)
-        books = [cb.rearrange("(p j) c -> p j c", j=PACK), cb2.rearrange("(p j) c -> p j c", j=PACK)]
-        lists_hbm = [offs, offs2]
+        z_planes = zT.rearrange("(p j) t -> p j t", j=PLANES)
+        dy_planes = dyT.rearrange("(p j) t -> p j t", j=PLANES)
+        book_planes = [book.rearrange("(p j) c -> p j c", j=PLANES) for book in (cb, cb2)]
 
-        lists = {}
-        book = {}
-        z_sb = {}
-        dy_sb = {}
-        dy4 = {}
-        diff = {}
-        pair_words = {}
-        back = {}
+        offsets = {}
+        window = {}
+        z_from = {}
+        dy_half = {}
+        dy4_from = {}
+        term = {}
+        turned_words = {}
+        back_bank = {}
         words = {}
+        g_piece = {}
+        g_codes = {}
+        w_codes = {}
 
         def load_list(b):
-            lists[b] = keep.tile([P, T // 16], U16, name="list%d" % b)
-            nc.sync.dma_start(lists[b][:], lists_hbm[b])
+            offsets[b] = sbuf.tile([P, T // LIST_ROWS], U16, name="offsets%d" % b)
+            nc.sync.dma_start(offsets[b][:], (offs, offs2)[b])
 
         def load_book(b, j):
-            book[b, j] = keep.tile([P, WINDOW[b]], F32, name="book%d_%d" % (b, j))
-            nc.vector.memset(book[b, j][:, C:], 0.0)
-            nc.sync.dma_start(book[b, j][:, :C], books[b][:, j, :])
+            window[b, j] = sbuf.tile([P, WINDOW[b]], F32, name="window%d_%d" % (b, j))
+            nc.vector.memset(window[b, j][:, C:], 0.0)
+            nc.sync.dma_start(window[b, j][:, :C], book_planes[b][:, j, :])
 
-        def load_z(j, q0, nq):
-            z_tile = keep.tile([P, nq * QT], F32, name="z%d_%d" % (j, q0))
-            nc.sync.dma_start(z_tile[:], z_pl[:, j, q0 * QT:(q0 + nq) * QT])
-            for i in range(2 * nq):
-                z_sb[j, 2 * q0 + i] = z_tile[:, i * P:]
+        def load_z(j, tb0, blocks):
+            z_tile = sbuf.tile([P, blocks * P], F32, name="z%d_%d" % (j, tb0))
+            nc.sync.dma_start(z_tile[:], z_planes[:, j, tb0 * P:(tb0 + blocks) * P])
+            for i in range(blocks):
+                z_from[j, tb0 + i] = z_tile[:, i * P:]
 
-        def load_dy(j, q0, nq):
-            dy_sb[j, q0] = keep.tile([P, nq * QT], F32, name="dy%d_%d" % (j, q0), tag="dy%d_%d" % (j, q0), align_bytes=64)
-            nc.sync.dma_start(dy_sb[j, q0][:], dy_pl[:, j, q0 * QT:(q0 + nq) * QT])
+        def load_dy(j, h):
+            dy_half[j, h] = sbuf.tile([P, HALF], F32, name="dy%d_%d" % (j, h), tag="dy%d_%d" % (j, h), align_bytes=64)
+            nc.sync.dma_start(dy_half[j, h][:], dy_planes[:, j, h * HALF:(h + 1) * HALF])
 
-        def load_pair(name, planes, u, q0, nq):
-            pair = keep.tile([P, 2, nq * QT], F32, name=name, tag=name, align_bytes=64)
-            nc.sync.dma_start(pair[:], planes[:, 2 * u:2 * u + 2, q0 * QT:(q0 + nq) * QT])
-            return pair
+        def load_last(name, planes):
+            last = sbuf.tile([P, 2, HALF], F32, name=name, tag=name, align_bytes=64)
+            nc.sync.dma_start(last[:], planes[:, 2:4, HALF:])
+            return last
 
-        w_raw = keep.tile([P, PACK, D], F32, name="w_raw")
-
-        def load_w():
-            nc.sync.dma_start(w_raw[:], wm.rearrange("(p j) d -> p j d", j=PACK))
-
+        w_raw = sbuf.tile([P, PLANES, D], F32, name="w_raw")
 
         load_book(0, 0)
         load_list(0)
         load_z(0, 0, 2)
         load_z(0, 2, 2)
-        load_dy(0, 0, 2)
+        load_z(0, 4, 4)
+        load_dy(0, 0)
         load_list(1)
         load_book(1, 0)
-        load_dy(0, 2, 2)
+        load_dy(0, 1)
         load_book(0, 1)
-        load_z(1, 0, 2)
-        load_dy(1, 0, 2)
+        load_z(1, 0, 4)
+        load_dy(1, 0)
         load_book(1, 1)
-        load_z(1, 2, 2)
-        load_dy(1, 2, 2)
+        load_z(1, 4, 4)
+        load_dy(1, 1)
         load_book(0, 2)
-        load_z(2, 0, 2)
-        load_dy(2, 0, 2)
+        load_z(2, 0, 4)
+        load_dy(2, 0)
         load_book(1, 2)
-        load_dy(3, 0, 2)
+        load_dy(3, 0)
         load_book(0, 3)
-        load_z(3, 0, 2)
+        load_z(3, 0, 4)
         load_book(1, 3)
-        z_high = load_pair("z_high", z_pl, 1, 2, 2)
-        load_w()
-        dy_high = load_pair("dy_high", dy_pl, 1, 2, 2)
+        z_last = load_last("z_last", z_planes)
+        nc.sync.dma_start(w_raw[:], wm.rearrange("(p j) d -> p j d", j=PLANES))
+        dy_last = load_last("dy_last", dy_planes)
 
-        def scale_dy(j, q0, first, nq):
-            scaled = keep.tile([P, nq * QT], F32, name="dy4_%d_%d" % (j, q0 + first), tag="dy4_%d_%d" % (j, q0 + first), align_bytes=64)
-            nc.scalar.activation(out=scaled[:], in_=dy_sb[j, q0][:, first * QT:(first + nq) * QT], func=COPY, scale=-1.0 / BETA)
-            for i in range(2 * nq):
-                dy4[j, 2 * (q0 + first) + i] = scaled[:, i * P:]
+        def scale_dy(j, h):
+            scaled = sbuf.tile([P, HALF], F32, name="dy4_%d_%d" % (j, h), align_bytes=64)
+            nc.scalar.activation(out=scaled[:], in_=dy_half[j, h][:], func=COPY, scale=-1.0 / BETA)
+            for i in range(HALF // P):
+                dy4_from[j, h * (HALF // P) + i] = scaled[:, i * P:]
 
-        def gather(b, j, tb0, ntb, into=None, other=None):
-            width = ntb * P
-            if into is None:
-                fresh = keep.tile([P, width], F32, name="diff%d_%d_%d" % (b, j, tb0))
-                into = fresh[:]
-            for i in range(ntb):
-                diff[b, j, tb0 + i] = into[:, i * P:(i + 1) * P]
-            window = book[b, j][:].indirect(lists[b][:, tb0 * (P // 16):(tb0 + ntb) * (P // 16)])
-            if other is None:
-                other = (z_sb, dy4)[b][j, tb0][:, :width]
-            nc.vector.tensor_tensor(into, window, other, (SUB, ADD)[b])
+        def gather_into(result, b, j, tb0, blocks, other):
+            columns = slice(tb0 * (P // LIST_ROWS), (tb0 + blocks) * (P // LIST_ROWS))
+            nc.vector.tensor_tensor(result, window[b, j][:].indirect(offsets[b][:, columns]), other, (SUB, ADD)[b])
 
-        def add_up(u, tb0, ntb, bank_tag, into=None, on_vector=False, order=(1, 0), planes=(1, 0)):
-            bank = psum.tile([P, ntb, 2, P], F32, name="sum%d_%d" % (u, tb0), tag=bank_tag)
-            for e in planes:
-                for i in range(ntb):
-                    for b in order:
+        def gather(b, j, tb0, blocks):
+            result = sbuf.tile([P, blocks * P], F32, name="term%d_%d_%d" % (b, j, tb0))
+            for i in range(blocks):
+                term[b, j, tb0 + i] = result[:, i * P:(i + 1) * P]
+            gather_into(result[:], b, j, tb0, blocks, (z_from, dy4_from)[b][j, tb0][:, :blocks * P])
+
+        def add_up(u, tb0, bank_tag, rounded, books):
+            bank = psum.tile([P, 2, 2, P], F32, name="sum%d_%d" % (u, tb0), tag=bank_tag)
+            for e in range(2):
+                for i in range(2):
+                    for b in books:
                         nc.tensor.matmul(
                             bank[:, i, e, :],
-                            lhsT=diff[b, 2 * u + e, tb0 + i],
+                            lhsT=term[b, 2 * u + e, tb0 + i],
                             rhs=ident[:],
                             is_transpose=True,
-                            start=(b == order[0]),
-                            stop=(b == order[1]),
+                            start=(b == books[0]),
+                            stop=(b == books[1]),
                         )
-            if into is None:
-                fresh = keep.tile([P, ntb * 2 * P], BF16, name="pairs%d_%d" % (u, tb0))
-                into = fresh[:]
-            for i in range(ntb):
-                pair_words[u, tb0 + i] = into[:, i * 2 * P:(i + 1) * 2 * P]
-            dst = into.rearrange("t (b p e) -> t b p e", b=ntb, e=2)
-            src = bank[:].rearrange("t b e p -> t b p e")
-            if on_vector:
-                nc.vector.tensor_scalar_mul(dst, src, -BETA)
-            else:
-                nc.scalar.activation(out=dst, in_=src, func=COPY, scale=-BETA)
-
-        def turn_back(u, tb0, ntb, bank_tag=None):
-            if u == 0:
-                back[tb0] = psum.tile([P, 2, ntb * P], F32, name="back%d" % tb0, tag=bank_tag)
-            for i in range(ntb):
-                nc.tensor.transpose(back[tb0][:, u, i * P:(i + 1) * P], pair_words[u, tb0 + i].bitcast(F32), ident[:])
-
-        def keep_words(tb0, ntb, first):
-            words[tb0] = keep.tile([P, 2, ntb * P], F32, name="words%d" % tb0)
-            nc.scalar.copy(out=words[tb0][:, 0, :], in_=back[first][:, 0, (tb0 - first) * P:(tb0 - first + ntb) * P])
-
-        def pair_up(u, tb0, ntb, minus_e, dy_pair):
-            nc.vector.scalar_tensor_tensor(
-                out=words[tb0][:, u, :].bitcast(BF16).rearrange("p (t e) -> p t e", e=2),
-                in0=minus_e.rearrange("p e t -> p t e"),
-                scalar=-BETA,
-                in1=dy_pair.rearrange("p e t -> p t e"),
-                op0=MULT,
-                op1=ADD,
+            for i in range(2):
+                turned_words[u, tb0 + i] = rounded[:, i * 2 * P:(i + 1) * 2 * P].bitcast(F32)
+            nc.scalar.activation(
+                out=rounded.rearrange("t (i p e) -> t i p e", i=2, e=2),
+                in_=bank[:].rearrange("t i e p -> t i p e"),
+                func=COPY,
+                scale=-BETA,
             )
 
-        def weave_words(tb0, ntb, on_vector):
-            g_bf[tb0] = keep.tile([P, ntb * P * PACK], BF16, name="g_bf%d" % tb0, align_bytes=64)
-            dst = g_bf[tb0][:].bitcast(F32).rearrange("p (t u) -> p t u", u=2)
-            src = words[tb0][:].rearrange("p u t -> p t u")
-            if on_vector:
-                nc.vector.tensor_copy(out=dst, in_=src)
-            else:
-                nc.scalar.copy(out=dst, in_=src)
+        def turn_back(u, tb0):
+            for i in range(2):
+                nc.tensor.transpose(back_bank[tb0][:, u, i * P:(i + 1) * P], turned_words[u, tb0 + i], ident[:])
 
-        g_codes = {}
-        g_scales = [keep.tile([P, HT], U8, name="g_scales%d" % h, align_bytes=64) for h in range(2)]
-        g_bf = {}
+        def open_back_bank(tb0, bank_tag):
+            back_bank[tb0] = psum.tile([P, 2, QUARTER], F32, name="back%d" % tb0, tag=bank_tag)
 
-        def weave(tb0, ntb, tag=None, on_vector=False):
-            g_bf[tb0] = keep.tile([P, ntb * P * PACK], BF16, name="g_bf%d" % tb0, tag=tag or "g_bf%d" % tb0, align_bytes=64)
-            dst = g_bf[tb0][:].bitcast(F32).rearrange("p (t u) -> p t u", u=2)
-            src = back[tb0][:].rearrange("p u t -> p t u")
-            if on_vector:
-                nc.vector.tensor_copy(out=dst, in_=src)
-            else:
-                nc.scalar.copy(out=dst, in_=src)
+        def keep_low_words(tb0, blocks):
+            first = (tb0 % 2) * P
+            words[tb0] = sbuf.tile([P, 2, blocks * P], F32, name="words%d" % tb0)
+            nc.scalar.copy(out=words[tb0][:, 0, :], in_=back_bank[tb0 - tb0 % 2][:, 0, first:first + blocks * P])
 
-        def quantise_g(tb0, ntb):
-            h = tb0 // 4
-            cols = slice((tb0 % 4) * P, (tb0 % 4 + ntb) * P)
-            nc.vector.quantize_mx(out=g_codes[h][:, cols].bitcast(E5), scales=g_scales[h][:, cols], in_=g_bf[tb0][:])
+        g_scales = [sbuf.tile([P, HALF], U8, name="g_scales%d" % h, align_bytes=64) for h in range(2)]
+        g_first = sbuf.tile([P, HALF * PLANES], BF16, name="g_first", align_bytes=64)
+        w_scales = sbuf.tile([P, D], U8, name="w_scales", align_bytes=64)
 
-        w_bf = {}
-        w_codes = {}
-        w_scales = keep.tile([P, D], U8, name="w_scales", align_bytes=64)
-
-        def cast_w(m):
+        def weave_first(tb0):
             nc.scalar.copy(
-                out=w_bf[0][:, m * P * PACK:(m + 1) * P * PACK].rearrange("p (c i j) -> p c j i", i=4, j=PACK),
+                out=g_first[:, tb0 * P * PLANES:(tb0 + 2) * P * PLANES].bitcast(F32).rearrange("p (t u) -> p t u", u=2),
+                in_=back_bank[tb0][:].rearrange("p u t -> p t u"),
+            )
+
+        def quantise_w(m):
+            columns = slice(m * P * PLANES, (m + 1) * P * PLANES)
+            nc.scalar.copy(
+                out=w_bf[:, columns].rearrange("p (c i j) -> p c j i", i=4, j=PLANES),
                 in_=w_raw[:, :, m * P:(m + 1) * P].rearrange("p j (c i) -> p c j i", i=4),
             )
+            w_codes[m] = sbuf.tile([P, P], U32, name="w_codes%d" % m, align_bytes=64)
+            nc.vector.quantize_mx(out=w_codes[m][:].bitcast(E4M3X4), scales=w_scales[:, m * P:(m + 1) * P], in_=w_bf[:, columns])
 
-        def quantise_w(m0, nm, tag=None):
-            codes = keep.tile([P, nm * P], U32, name="w_codes%d" % m0, tag=tag or "w_codes%d" % m0, align_bytes=64)
-            first = m0 * P * PACK
-            nc.vector.quantize_mx(
-                out=codes[:].bitcast(E4),
-                scales=w_scales[:, m0 * P:(m0 + nm) * P],
-                in_=w_bf[0][:, first:first + nm * P * PACK],
-            )
-            for i in range(nm):
-                w_codes[m0 + i] = codes[:, i * P:(i + 1) * P]
-
-        def multiply(h, m, bank_tag, on_vector):
-            acc = psum.tile([P, HT], F32, name="acc%d_%d" % (h, m), tag=bank_tag)
+        def multiply(h, m, bank_tag, copy_out):
+            acc = psum.tile([P, HALF], F32, name="acc%d_%d" % (h, m), tag=bank_tag)
             nc.tensor.matmul_mx(
                 out=acc[:],
-                lhsT=w_codes[m].bitcast(E4),
+                lhsT=w_codes[m][:].bitcast(E4M3X4),
                 lhsT_scale=w_scales[:, m * P:(m + 1) * P],
-                rhs=g_codes[h][:].bitcast(E5),
+                rhs=g_codes[h][:].bitcast(E5M2X4),
                 rhs_scale=g_scales[h][:],
                 start=True,
                 stop=True,
             )
-            res = keep.tile([P, HT], F32, name="res%d_%d" % (h, m))
-            if on_vector:
-                nc.vector.tensor_copy(out=res[:], in_=acc[:])
-            else:
-                nc.scalar.copy(out=res[:], in_=acc[:])
-            nc.sync.dma_start(out[m * P:(m + 1) * P, h * HT:(h + 1) * HT], res[:])
+            result = sbuf.tile([P, HALF], F32, name="out%d_%d" % (h, m))
+            copy_out(out=result[:], in_=acc[:])
+            nc.sync.dma_start(out[m * P:(m + 1) * P, h * HALF:(h + 1) * HALF], result[:])
 
-        scale_dy(0, 0, 0, 2)
-        scale_dy(0, 2, 0, 2)
-        scale_dy(1, 0, 0, 2)
-        scale_dy(1, 2, 0, 2)
-        gather(0, 0, 0, 4)
+        for j in range(2):
+            for h in range(2):
+                scale_dy(j, h)
+        gather(0, 0, 0, 2)
+        gather(0, 0, 2, 2)
         gather(0, 0, 4, 4)
         gather(1, 0, 0, 4)
         gather(1, 0, 4, 4)
-        gather(0, 1, 0, 4)
-        gather(1, 1, 0, 4)
-        gather(0, 1, 4, 4)
-        gather(1, 1, 4, 4)
-        low_pairs = keep.tile([P, 2, 2 * QT], BF16, name="low_pairs", tag="dy1_2", align_bytes=64)
+        for tb0 in (0, 4):
+            for b in range(2):
+                gather(b, 1, tb0, 4)
+        rounded_low_first = sbuf.tile([P, 2, 2 * QUARTER], BF16, name="rounded_low_first", tag="dy1_1", align_bytes=64)
         for q in range(2):
-            add_up(0, 2 * q, 2, "out%d" % q, low_pairs[:, q, :], False, (0, 1), (0, 1))
-            turn_back(0, 2 * q, 2, "back%d" % q)
-        scale_dy(2, 0, 0, 2)
-        low_pairs2 = keep.tile([P, 2, 2 * QT], BF16, name="low_pairs2", tag="dy2_0", align_bytes=64)
+            add_up(0, 2 * q, "bank%d" % q, rounded_low_first[:, q, :], (0, 1))
+            open_back_bank(2 * q, "bank%d" % (4 + q))
+            turn_back(0, 2 * q)
+        scale_dy(2, 0)
+        rounded_low_second = sbuf.tile([P, 2, 2 * QUARTER], BF16, name="rounded_low_second", tag="dy2_0", align_bytes=64)
         for q in range(2, 4):
-            add_up(0, 2 * q, 2, "sum%d" % (q - 2), low_pairs2[:, q - 2, :], False, (0, 1), (0, 1))
-        turn_back(0, 4, 2, "back2")
-        turn_back(0, 6, 2, "back3")
-        scale_dy(3, 0, 0, 2)
-        keep_words(4, 2, 4)
-        keep_words(6, 1, 6)
-        keep_words(7, 1, 6)
+            add_up(0, 2 * q, "bank%d" % q, rounded_low_second[:, q - 2, :], (0, 1))
+        for q in range(2, 4):
+            open_back_bank(2 * q, "bank%d" % (4 + q))
+            turn_back(0, 2 * q)
+        scale_dy(3, 0)
+        last_pieces = ((4, 2), (6, 1), (7, 1))
+        for tb0, blocks in last_pieces:
+            keep_low_words(tb0, blocks)
+
         gather(0, 2, 0, 4)
         gather(1, 2, 0, 4)
         gather(0, 3, 0, 4)
         gather(1, 3, 0, 2)
         gather(1, 3, 2, 2)
-        high_pairs = keep.tile([P, 2, 2 * QT], BF16, name="high_pairs", tag="high_pairs", align_bytes=64)
+        rounded_high = sbuf.tile([P, 2, 2 * QUARTER], BF16, name="rounded_high", tag="rounded_high", align_bytes=64)
         for q in range(2):
-            add_up(1, 2 * q, 2, "out%d" % q, high_pairs[:, q, :], False, (1, 0), (0, 1))
-            turn_back(1, 2 * q, 2)
-        weave(0, 2)
-        weave(2, 2)
-        w_bf[0] = keep.tile([P, D * PACK], BF16, name="w_bf", tag="high_pairs", align_bytes=64)
-        part = keep.tile([P, 2, HT], F32, name="part")
+            add_up(1, 2 * q, "bank%d" % q, rounded_high[:, q, :], (1, 0))
+            turn_back(1, 2 * q)
+        for q in range(2):
+            weave_first(2 * q)
+
+        w_bf = sbuf.tile([P, D * PLANES], BF16, name="w_bf", tag="rounded_high", align_bytes=64)
+        cb_minus_z = sbuf.tile([P, 2, HALF], F32, name="cb_minus_z")
+        minus_e = sbuf.tile([P, 2, HALF], F32, name="minus_e")
+
+        def piece_columns(tb0, blocks):
+            return slice(tb0 * P - HALF, (tb0 + blocks) * P - HALF)
+
+        def gather_last(tb0, blocks):
+            columns = piece_columns(tb0, blocks)
+            gather_into(minus_e[:, 1, columns], 1, 3, tb0, blocks, cb_minus_z[:, 1, columns])
+
         for e in range(2):
-            gather(0, 2 + e, 4, 4, part[:, e, :], z_high[:, e, :])
-        minus_third = keep.tile([P, 2, QT], F32, name="minus_third")
-        for e in range(2):
-            gather(1, 2 + e, 4, 2, minus_third[:, e, :], part[:, e, :QT])
-        g_codes[0] = keep.tile([P, HT], U32, name="g_codes0", tag="z_high", align_bytes=64)
-        quantise_g(0, 2)
-        quantise_g(2, 2)
-        minus_last = keep.tile([P, 2, QT], F32, name="minus_last")
-        cast_w(0)
-        quantise_w(0, 1)
-        cast_w(1)
-        quantise_w(1, 1)
-        gather(1, 2, 6, 2, minus_last[:, 0, :], part[:, 0, QT:])
-        for i in range(2):
-            gather(1, 3, 6 + i, 1, minus_last[:, 1, i * P:(i + 1) * P], part[:, 1, QT + i * P:QT + (i + 1) * P])
-        multiply(0, 0, "sum0", False)
-        cast_w(2)
-        quantise_w(2, 1)
-        multiply(0, 1, "sum1", False)
-        cast_w(3)
-        quantise_w(3, 1)
-        pair_up(1, 4, 2, minus_third[:], dy_high[:, :, :QT])
-        for i in range(2):
-            pair_up(1, 6 + i, 1, minus_last[:, :, i * P:(i + 1) * P], dy_high[:, :, QT + i * P:QT + (i + 1) * P])
-        g_codes[1] = keep.tile([P, HT], U32, name="g_codes1", align_bytes=64)
-        weave_words(4, 2, True)
-        for i in range(2):
-            weave_words(6 + i, 1, True)
-        quantise_g(4, 2)
-        for i in range(2):
-            quantise_g(6 + i, 1)
-        multiply(0, 2, "back2", False)
-        multiply(0, 3, "back3", False)
-        for m, tag in enumerate(("out0", "out1", "back0", "back1")):
-            multiply(1, m, tag, m % 2 == 0)
+            gather_into(cb_minus_z[:, e, :], 0, 2 + e, 4, 4, z_last[:, e, :])
+        gather_into(minus_e[:, 0, :], 1, 2, 4, 4, cb_minus_z[:, 0, :])
+        gather_last(*last_pieces[0])
+        g_codes[0] = sbuf.tile([P, HALF], U32, name="g_codes0", tag="z_last", align_bytes=64)
+        nc.vector.quantize_mx(out=g_codes[0][:].bitcast(E5M2X4), scales=g_scales[0][:], in_=g_first[:])
+        quantise_w(0)
+        quantise_w(1)
+        for piece in last_pieces[1:]:
+            gather_last(*piece)
+        multiply(0, 0, "bank2", nc.scalar.copy)
+        quantise_w(2)
+        multiply(0, 1, "bank3", nc.scalar.copy)
+        quantise_w(3)
+        for tb0, blocks in last_pieces:
+            columns = piece_columns(tb0, blocks)
+            nc.vector.scalar_tensor_tensor(
+                out=words[tb0][:, 1, :].bitcast(BF16).rearrange("p (t e) -> p t e", e=2),
+                in0=minus_e[:, :, columns].rearrange("p e t -> p t e"),
+                scalar=-BETA,
+                in1=dy_last[:, :, columns].rearrange("p e t -> p t e"),
+                op0=MULT,
+                op1=ADD,
+            )
+        g_codes[1] = sbuf.tile([P, HALF], U32, name="g_codes1", align_bytes=64)
+        for tb0, blocks in last_pieces:
+            g_piece[tb0] = sbuf.tile([P, blocks * P * PLANES], BF16, name="g_piece%d" % tb0, align_bytes=64)
+            nc.vector.tensor_copy(
+                out=g_piece[tb0][:].bitcast(F32).rearrange("p (t u) -> p t u", u=2),
+                in_=words[tb0][:].rearrange("p u t -> p t u"),
+            )
+        for tb0, blocks in last_pieces:
+            columns = piece_columns(tb0, blocks)
+            nc.vector.quantize_mx(out=g_codes[1][:, columns].bitcast(E5M2X4), scales=g_scales[1][:, columns], in_=g_piece[tb0][:])
+        multiply(0, 2, "bank6", nc.scalar.copy)
+        multiply(0, 3, "bank7", nc.scalar.copy)
+
+        for m, bank_tag in enumerate(("bank0", "bank1", "bank4", "bank5")):
+            multiply(1, m, bank_tag, (nc.vector.tensor_copy, nc.scalar.copy)[m % 2])

from contextlib import ExitStack

import concourse.mybir as mybir
from concourse.masks import make_identity

T, C, D, DV = 1024, 512, 512, 512
BETA = 0.25
FLOPS = 2 * DV * D * T

F32 = mybir.dt.float32
BF16 = mybir.dt.bfloat16
U32 = mybir.dt.uint32
U16 = mybir.dt.uint16
U8 = mybir.dt.uint8
E4M3X4 = mybir.dt.float8_e4m3fn_x4
E5M2X4 = mybir.dt.float8_e5m2_x4
SUB = mybir.AluOpType.subtract
ADD = mybir.AluOpType.add
MULT = mybir.AluOpType.mult
COPY = mybir.ActivationFunctionType.Copy

P = 128
PLANES = 4
QUARTER = 256
HALF = 512
LIST_ROWS = 16
WINDOW = (2 * C, C + 64)


def tile_attend_gvq_rs_x_kernel(tc, zT, cb, cb2, dyT, wm, offs, offs2, out):
    nc = tc.nc
    with ExitStack() as ctx:
        sbuf = ctx.enter_context(tc.tile_pool(name="sbuf", bufs=1))
        psum = ctx.enter_context(tc.psum_pool(name="psum", bufs=1))

        ident = sbuf.tile([P, P], F32, name="ident")
        make_identity(nc, ident[:])

        z_planes = zT.rearrange("(p j) t -> p j t", j=PLANES)
        dy_planes = dyT.rearrange("(p j) t -> p j t", j=PLANES)
        book_planes = [book.rearrange("(p j) c -> p j c", j=PLANES) for book in (cb, cb2)]

        offsets = {}
        window = {}
        z_from = {}
        dy_half = {}
        dy4_from = {}
        term = {}
        turned_words = {}
        back_bank = {}
        words = {}
        g_piece = {}
        g_codes = {}
        w_codes = {}

        def load_list(b):
            offsets[b] = sbuf.tile([P, T // LIST_ROWS], U16, name="offsets%d" % b)
            nc.sync.dma_start(offsets[b][:], (offs, offs2)[b])

        def load_book(b, j):
            window[b, j] = sbuf.tile([P, WINDOW[b]], F32, name="window%d_%d" % (b, j))
            nc.vector.memset(window[b, j][:, C:], 0.0)
            nc.sync.dma_start(window[b, j][:, :C], book_planes[b][:, j, :])

        def load_z(j, tb0, blocks):
            z_tile = sbuf.tile([P, blocks * P], F32, name="z%d_%d" % (j, tb0))
            nc.sync.dma_start(z_tile[:], z_planes[:, j, tb0 * P:(tb0 + blocks) * P])
            for i in range(blocks):
                z_from[j, tb0 + i] = z_tile[:, i * P:]

        def load_dy(j, h):
            dy_half[j, h] = sbuf.tile([P, HALF], F32, name="dy%d_%d" % (j, h), tag="dy%d_%d" % (j, h), align_bytes=64)
            nc.sync.dma_start(dy_half[j, h][:], dy_planes[:, j, h * HALF:(h + 1) * HALF])

        def load_last(name, planes):
            last = sbuf.tile([P, 2, HALF], F32, name=name, tag=name, align_bytes=64)
            nc.sync.dma_start(last[:], planes[:, 2:4, HALF:])
            return last

        w_raw = sbuf.tile([P, PLANES, D], F32, name="w_raw")

        load_book(0, 0)
        load_list(0)
        load_z(0, 0, 2)
        load_z(0, 2, 2)
        load_z(0, 4, 4)
        load_dy(0, 0)
        load_list(1)
        load_book(1, 0)
        load_dy(0, 1)
        load_book(0, 1)
        load_z(1, 0, 4)
        load_dy(1, 0)
        load_book(1, 1)
        load_z(1, 4, 4)
        load_dy(1, 1)
        load_book(0, 2)
        load_z(2, 0, 4)
        load_dy(2, 0)
        load_book(1, 2)
        load_dy(3, 0)
        load_book(0, 3)
        load_z(3, 0, 4)
        load_book(1, 3)
        z_last = load_last("z_last", z_planes)
        nc.sync.dma_start(w_raw[:], wm.rearrange("(p j) d -> p j d", j=PLANES))
        dy_last = load_last("dy_last", dy_planes)

        def scale_dy(j, h):
            scaled = sbuf.tile([P, HALF], F32, name="dy4_%d_%d" % (j, h), align_bytes=64)
            nc.scalar.activation(out=scaled[:], in_=dy_half[j, h][:], func=COPY, scale=-1.0 / BETA)
            for i in range(HALF // P):
                dy4_from[j, h * (HALF // P) + i] = scaled[:, i * P:]

        def gather_into(result, b, j, tb0, blocks, other):
            columns = slice(tb0 * (P // LIST_ROWS), (tb0 + blocks) * (P // LIST_ROWS))
            nc.vector.tensor_tensor(result, window[b, j][:].indirect(offsets[b][:, columns]), other, (SUB, ADD)[b])

        def gather(b, j, tb0, blocks):
            result = sbuf.tile([P, blocks * P], F32, name="term%d_%d_%d" % (b, j, tb0))
            for i in range(blocks):
                term[b, j, tb0 + i] = result[:, i * P:(i + 1) * P]
            gather_into(result[:], b, j, tb0, blocks, (z_from, dy4_from)[b][j, tb0][:, :blocks * P])

        def add_up(u, tb0, bank_tag, rounded, books):
            bank = psum.tile([P, 2, 2, P], F32, name="sum%d_%d" % (u, tb0), tag=bank_tag)
            for e in range(2):
                for i in range(2):
                    for b in books:
                        nc.tensor.matmul(
                            bank[:, i, e, :],
                            lhsT=term[b, 2 * u + e, tb0 + i],
                            rhs=ident[:],
                            is_transpose=True,
                            start=(b == books[0]),
                            stop=(b == books[1]),
                        )
            for i in range(2):
                turned_words[u, tb0 + i] = rounded[:, i * 2 * P:(i + 1) * 2 * P].bitcast(F32)
            nc.scalar.activation(
                out=rounded.rearrange("t (i p e) -> t i p e", i=2, e=2),
                in_=bank[:].rearrange("t i e p -> t i p e"),
                func=COPY,
                scale=-BETA,
            )

        def turn_back(u, tb0):
            for i in range(2):
                nc.tensor.transpose(back_bank[tb0][:, u, i * P:(i + 1) * P], turned_words[u, tb0 + i], ident[:])

        def open_back_bank(tb0, bank_tag):
            back_bank[tb0] = psum.tile([P, 2, QUARTER], F32, name="back%d" % tb0, tag=bank_tag)

        def keep_low_words(tb0, blocks):
            first = (tb0 % 2) * P
            words[tb0] = sbuf.tile([P, 2, blocks * P], F32, name="words%d" % tb0)
            nc.scalar.copy(out=words[tb0][:, 0, :], in_=back_bank[tb0 - tb0 % 2][:, 0, first:first + blocks * P])

        g_scales = [sbuf.tile([P, HALF], U8, name="g_scales%d" % h, align_bytes=64) for h in range(2)]
        g_first = sbuf.tile([P, HALF * PLANES], BF16, name="g_first", align_bytes=64)
        w_scales = sbuf.tile([P, D], U8, name="w_scales", align_bytes=64)

        def weave_first(tb0):
            nc.scalar.copy(
                out=g_first[:, tb0 * P * PLANES:(tb0 + 2) * P * PLANES].bitcast(F32).rearrange("p (t u) -> p t u", u=2),
                in_=back_bank[tb0][:].rearrange("p u t -> p t u"),
            )

        def quantise_w(m):
            columns = slice(m * P * PLANES, (m + 1) * P * PLANES)
            nc.scalar.copy(
                out=w_bf[:, columns].rearrange("p (c i j) -> p c j i", i=4, j=PLANES),
                in_=w_raw[:, :, m * P:(m + 1) * P].rearrange("p j (c i) -> p c j i", i=4),
            )
            w_codes[m] = sbuf.tile([P, P], U32, name="w_codes%d" % m, align_bytes=64)
            nc.vector.quantize_mx(out=w_codes[m][:].bitcast(E4M3X4), scales=w_scales[:, m * P:(m + 1) * P], in_=w_bf[:, columns])

        def multiply(h, m, bank_tag, copy_out):
            acc = psum.tile([P, HALF], F32, name="acc%d_%d" % (h, m), tag=bank_tag)
            nc.tensor.matmul_mx(
                out=acc[:],
                lhsT=w_codes[m][:].bitcast(E4M3X4),
                lhsT_scale=w_scales[:, m * P:(m + 1) * P],
                rhs=g_codes[h][:].bitcast(E5M2X4),
                rhs_scale=g_scales[h][:],
                start=True,
                stop=True,
            )
            result = sbuf.tile([P, HALF], F32, name="out%d_%d" % (h, m))
            copy_out(out=result[:], in_=acc[:])
            nc.sync.dma_start(out[m * P:(m + 1) * P, h * HALF:(h + 1) * HALF], result[:])

        for j in range(2):
            for h in range(2):
                scale_dy(j, h)
        gather(0, 0, 0, 2)
        gather(0, 0, 2, 2)
        gather(0, 0, 4, 4)
        gather(1, 0, 0, 4)
        gather(1, 0, 4, 4)
        for tb0 in (0, 4):
            for b in range(2):
                gather(b, 1, tb0, 4)
        rounded_low_first = sbuf.tile([P, 2, 2 * QUARTER], BF16, name="rounded_low_first", tag="dy1_1", align_bytes=64)
        for q in range(2):
            add_up(0, 2 * q, "bank%d" % q, rounded_low_first[:, q, :], (0, 1))
            open_back_bank(2 * q, "bank%d" % (4 + q))
            turn_back(0, 2 * q)
        scale_dy(2, 0)
        rounded_low_second = sbuf.tile([P, 2, 2 * QUARTER], BF16, name="rounded_low_second", tag="dy2_0", align_bytes=64)
        for q in range(2, 4):
            add_up(0, 2 * q, "bank%d" % q, rounded_low_second[:, q - 2, :], (0, 1))
        for q in range(2, 4):
            open_back_bank(2 * q, "bank%d" % (4 + q))
            turn_back(0, 2 * q)
        scale_dy(3, 0)
        last_pieces = ((4, 2), (6, 1), (7, 1))
        for tb0, blocks in last_pieces:
            keep_low_words(tb0, blocks)

        gather(0, 2, 0, 4)
        gather(1, 2, 0, 4)
        gather(0, 3, 0, 4)
        gather(1, 3, 0, 2)
        gather(1, 3, 2, 2)
        rounded_high = sbuf.tile([P, 2, 2 * QUARTER], BF16, name="rounded_high", tag="rounded_high", align_bytes=64)
        for q in range(2):
            add_up(1, 2 * q, "bank%d" % q, rounded_high[:, q, :], (1, 0))
            turn_back(1, 2 * q)
        for q in range(2):
            weave_first(2 * q)

        w_bf = sbuf.tile([P, D * PLANES], BF16, name="w_bf", tag="rounded_high", align_bytes=64)
        cb_minus_z = sbuf.tile([P, 2, HALF], F32, name="cb_minus_z")
        minus_e = sbuf.tile([P, 2, HALF], F32, name="minus_e")

        def piece_columns(tb0, blocks):
            return slice(tb0 * P - HALF, (tb0 + blocks) * P - HALF)

        def gather_last(tb0, blocks):
            columns = piece_columns(tb0, blocks)
            gather_into(minus_e[:, 1, columns], 1, 3, tb0, blocks, cb_minus_z[:, 1, columns])

        for e in range(2):
            gather_into(cb_minus_z[:, e, :], 0, 2 + e, 4, 4, z_last[:, e, :])
        gather_into(minus_e[:, 0, :], 1, 2, 4, 4, cb_minus_z[:, 0, :])
        gather_last(*last_pieces[0])
        g_codes[0] = sbuf.tile([P, HALF], U32, name="g_codes0", tag="z_last", align_bytes=64)
        nc.vector.quantize_mx(out=g_codes[0][:].bitcast(E5M2X4), scales=g_scales[0][:], in_=g_first[:])
        quantise_w(0)
        quantise_w(1)
        for piece in last_pieces[1:]:
            gather_last(*piece)
        multiply(0, 0, "bank2", nc.scalar.copy)
        quantise_w(2)
        multiply(0, 1, "bank3", nc.scalar.copy)
        quantise_w(3)
        for tb0, blocks in last_pieces:
            columns = piece_columns(tb0, blocks)
            nc.vector.scalar_tensor_tensor(
                out=words[tb0][:, 1, :].bitcast(BF16).rearrange("p (t e) -> p t e", e=2),
                in0=minus_e[:, :, columns].rearrange("p e t -> p t e"),
                scalar=-BETA,
                in1=dy_last[:, :, columns].rearrange("p e t -> p t e"),
                op0=MULT,
                op1=ADD,
            )
        g_codes[1] = sbuf.tile([P, HALF], U32, name="g_codes1", align_bytes=64)
        for tb0, blocks in last_pieces:
            g_piece[tb0] = sbuf.tile([P, blocks * P * PLANES], BF16, name="g_piece%d" % tb0, align_bytes=64)
            nc.vector.tensor_copy(
                out=g_piece[tb0][:].bitcast(F32).rearrange("p (t u) -> p t u", u=2),
                in_=words[tb0][:].rearrange("p u t -> p t u"),
            )
        for tb0, blocks in last_pieces:
            columns = piece_columns(tb0, blocks)
            nc.vector.quantize_mx(out=g_codes[1][:, columns].bitcast(E5M2X4), scales=g_scales[1][:, columns], in_=g_piece[tb0][:])
        multiply(0, 2, "bank6", nc.scalar.copy)
        multiply(0, 3, "bank7", nc.scalar.copy)

        for m, bank_tag in enumerate(("bank0", "bank1", "bank4", "bank5")):
            multiply(1, m, bank_tag, (nc.vector.tensor_copy, nc.scalar.copy)[m % 2])
